import numpy as np
import ml_dtypes


def mxq(x, axis, fmt="e4m3"):
    dtype, down = {"e4m3": (ml_dtypes.float8_e4m3fn, 7), "e5m2": (ml_dtypes.float8_e5m2, 14)}[fmt]
    v = np.moveaxis(np.asarray(x, np.float32).astype(ml_dtypes.bfloat16).astype(np.float64), axis, -1)
    blocks = v.reshape(v.shape[:-1] + (-1, 32))
    amax = np.abs(blocks).max(-1, keepdims=True)
    byte = np.maximum(np.where(amax > 0, np.frexp(amax)[1] - 1 + 127, 0) - down, 1)
    scale = np.exp2(byte - 127.0)
    codes = (blocks / scale).astype(np.float32).astype(dtype).astype(np.float64)
    return np.moveaxis((codes * scale).reshape(v.shape), -1, axis)


WIDE = False


def mx_kscale(k):
    if not WIDE:
        return np.ones(k)
    levels = np.array([10, -10, 5, -5, 0])
    if k % 512:
        return np.exp2(np.random.permutation(np.resize(levels, k // 32))).repeat(32)
    a = np.empty((k // 512, 16))
    for p in range(k // 512):
        a[p, :8] = np.random.permutation(np.resize(levels, 8))
        for g in range(8):
            far = levels[np.abs(levels - a[p, g]) >= 10]
            a[p, g + 8] = far[np.random.randint(len(far))]
    return np.exp2(a.ravel()).repeat(32)


BF16 = ml_dtypes.bfloat16


def bf(x):
    return np.asarray(x, np.float32).astype(BF16)


def f64(x):
    return np.asarray(x).astype(np.float64)


E2M1 = np.array([0.0, 0.5, 1.0, 1.5, 2.0, 3.0, 4.0, 6.0, -0.0, -0.5, -1.0, -1.5, -2.0, -3.0, -4.0, -6.0])


def pack_weight(w, fmt):
    k, n = w.shape
    w = f64(bf(w)).reshape(k // 32, 32, n)
    amax = np.abs(w).max(1)
    if fmt == "e4m3":
        byte = np.frexp(amax)[1] - 1 + 127 - 7
    else:
        mant, ex = np.frexp(amax / 6.0)
        byte = np.where(mant > 0.5, ex, ex - 1) + 127
    byte = np.clip(np.where(amax > 0, byte, 1), 1, 254)
    scaled = (w * np.exp2(127.0 - byte)[:, None, :]).reshape(k, n).astype(np.float32)
    by_word = np.ascontiguousarray(scaled.reshape(k // 512, 128, 4, n).transpose(0, 1, 3, 2))
    if fmt == "e4m3":
        words = by_word.astype(ml_dtypes.float8_e4m3fn).view(np.uint8)
    else:
        c = by_word.astype(ml_dtypes.float4_e2m1fn).view(np.uint8) & 0xF
        words = c[..., 0::2] | (c[..., 1::2] << 4)
    return np.ascontiguousarray(words), np.ascontiguousarray(byte.astype(np.uint8).reshape(k // 512, 16, n))


def unpack_weight(words, scales, fmt):
    g, p, n, _ = words.shape
    if fmt == "e4m3":
        vals = np.ascontiguousarray(words).view(ml_dtypes.float8_e4m3fn).astype(np.float64)
    else:
        nib = np.empty((g, p, n, 4), np.uint8)
        nib[..., 0::2] = words & 0xF
        nib[..., 1::2] = words >> 4
        vals = E2M1[nib]
    vals = vals * np.repeat(np.exp2(scales.astype(np.float64) - 127.0), 8, axis=1)[..., None]
    return vals.transpose(0, 1, 3, 2).reshape(g * 512, n)
def pack4(w):
    words, scales = pack_weight(w, "e2m1")
    return words.reshape(words.shape[0], 128, -1), scales


def unpack4(words, scales):
    return unpack_weight(words.reshape(words.shape[0], 128, -1, 2), scales, "e2m1")


def planes(Y):
    n, m = Y.shape
    b = f64(bf(Y)).reshape(n // 32, 32, m)
    amax = np.abs(b).max(1)
    byte = np.clip(np.where(amax > 0, np.frexp(amax)[1] - 1 + 127 - 7, 1), 1, 254)
    codes = (b * np.exp2(127.0 - byte)[:, None, :]).reshape(n, m).astype(np.float32).astype(ml_dtypes.float8_e4m3fn).view(np.uint8)
    words = codes.reshape(n // 512, 128, 4, m).transpose(0, 1, 3, 2)
    return np.ascontiguousarray(words), np.ascontiguousarray(byte.astype(np.uint8).reshape(n // 512, 16, m))


S, KA, KB, R = 1024, 2048, 1024, 1024
BIAS = 0.3
SPREAD = 0.8


def setup_inputs():
    rnd = np.random.randn
    sa = mx_kscale(KA)
    sb = mx_kscale(KB)
    size = np.exp(SPREAD * rnd(R))
    a_words, a_scales = pack_weight(rnd(KA, S) * sa[:, None], "e4m3")
    b_words, b_scales = pack_weight(rnd(KB, S) * sb[:, None], "e4m3")
    U = bf(rnd(KA, R) / np.sqrt(KA) * size[None, :] / sa[:, None])
    V = bf(rnd(KB, R) / np.sqrt(KB) / sb[:, None])
    return {"a_words": a_words, "a_scales": a_scales,
            "b_words": b_words, "b_scales": b_scales,
            "U": U, "V": V,
            "bias_u": bf(BIAS * rnd(R) * size),
            "bias_v": bf(BIAS * rnd(R)),
            "bias_f": bf(BIAS * rnd(R) * size)}


def reference(a_words, a_scales, b_words, b_scales, U, V, bias_u, bias_v, bias_f):
    A = unpack_weight(a_words, a_scales, "e4m3")
    B = unpack_weight(b_words, b_scales, "e4m3")
    left = A.T @ mxq(f64(U), 0, "e4m3")
    right = B.T @ mxq(f64(V), 0, "e4m3")
    y = (left + f64(bias_u)) * (right + f64(bias_v)) + f64(bias_f)
    Y = y.T
    words, scales = planes(Y)
    return y, words, scales

from contextlib import ExitStack

import concourse.mybir as mybir
from concourse.masks import make_identity

S, KA, KB, R = 1024, 2048, 1024, 1024
FLOPS = 2 * S * R * (KA + KB)

F32 = mybir.dt.float32
BF16 = mybir.dt.bfloat16
I32 = mybir.dt.int32
U32 = mybir.dt.uint32
U8 = mybir.dt.uint8
FP8X4 = mybir.dt.float8_e4m3fn_x4
ADD = mybir.AluOpType.add
MULT = mybir.AluOpType.mult
IDENTITY = mybir.ActivationFunctionType.Identity

P = 128
PACK = 4
W = 512
BANKS = 8
UNITS = [(0, 0, 512), (0, 512, 512), (1, 0, 512), (1, 512, 256), (1, 768, 256)]
LOADS = [('V', 0, 0), ('B', 0, 0), ('V', 0, 1), ('B', 1, 0), ('B', 0, 1), ('B', 1, 1), ('V', 1, 0), ('V', 1, 1), ('U', 0, 0), ('A', 0, 0), ('U', 0, 1), ('A', 1, 0), ('U', 0, 2), ('A', 2, 0), ('U', 0, 3), ('A', 3, 0), ('A', 0, 1), ('A', 1, 1), ('U', 1, 0), ('A', 2, 1), ('A', 3, 1), ('U', 1, 1), ('U', 1, 2), ('U', 1, 3)]
PLAN = [
    ('W', ('V', 0, 0), 'V', 0, 96),
    ('W', ('V', 0, 0), 'S', 96, 128),
    ('Q', ('V', 0, 0), 0, 1),
    ('Q', ('V', 0, 0), 1, 2),
    ('Q', ('V', 0, 0), 3, 4),
    ('mm', 'V', 0, 0, 512, 0, 0, 0),
    ('Q', ('V', 0, 0), 2, 3),
    ('W', ('V', 0, 1), 'V', 0, 96),
    ('W', ('V', 0, 1), 'S', 96, 128),
    ('mm', 'V', 0, 0, 512, 1, 0, 1),
    ('mm', 'V', 0, 0, 512, 2, 0, 2),
    ('Q', ('V', 0, 1), 0, 4),
    ('mm', 'V', 0, 0, 512, 3, 0, 3),
    ('bt', 4),
    ('mm', 'V', 0, 0, 512, 0, 1, 0),
    ('bo',),
    ('mm', 'V', 0, 0, 512, 1, 1, 1),
    ('e1', 'V', 0, 0, 0),
    ('mm', 'V', 0, 0, 512, 2, 1, 2),
    ('e1', 'S', 0, 0, 1),
    ('mm', 'V', 0, 0, 512, 3, 1, 3),
    ('W', ('V', 1, 0), 'V', 0, 128),
    ('mm', 'V', 0, 512, 512, 0, 0, 5),
    ('mm', 'V', 0, 512, 512, 0, 1, 5),
    ('e1', 'S', 0, 0, 3),
    ('mm', 'V', 0, 512, 512, 1, 0, 6),
    ('mm', 'V', 0, 512, 512, 1, 1, 6),
    ('W', ('V', 1, 1), 'S', 48, 128),
    ('mm', 'V', 0, 512, 512, 2, 0, 7),
    ('W', ('V', 1, 1), 'V', 0, 48),
    ('mm', 'V', 0, 512, 512, 2, 1, 7),
    ('mm', 'V', 0, 512, 512, 3, 0, 4),
    ('Q', ('V', 1, 0), 0, 4),
    ('mm', 'V', 0, 512, 512, 3, 1, 4),
    ('W', ('U', 0, 0), 'V', 0, 112),
    ('e1', 'S', 0, 0, 2),
    ('mm', 'V', 1, 0, 512, 0, 0, 0),
    ('mm', 'V', 1, 0, 512, 1, 0, 1),
    ('W', ('U', 0, 0), 'S', 112, 128),
    ('mm', 'V', 1, 0, 512, 2, 0, 3),
    ('e1', 'S', 0, 1, 2),
    ('mm', 'V', 1, 0, 512, 3, 0, 2),
    ('Q', ('V', 1, 1), 0, 4),
    ('e1', 'S', 0, 1, 1),
    ('W', ('U', 0, 1), 'V', 0, 96),
    ('mm', 'V', 1, 0, 512, 0, 1, 0),
    ('W', ('U', 0, 1), 'S', 96, 128),
    ('mm', 'V', 1, 0, 512, 1, 1, 1),
    ('mm', 'V', 1, 0, 512, 2, 1, 3),
    ('e1', 'S', 0, 1, 3),
    ('Q', ('U', 0, 0), 0, 4),
    ('mm', 'V', 1, 0, 512, 3, 1, 2),
    ('mm', 'V', 1, 512, 512, 0, 0, 7),
    ('e1', 'S', 0, 1, 0),
    ('Q', ('U', 0, 1), 0, 4),
    ('mm', 'V', 1, 512, 512, 0, 1, 7),
    ('mm', 'V', 1, 512, 512, 1, 0, 6),
    ('e1', 'S', 1, 0, 1),
    ('W', ('U', 0, 2), 'V', 0, 112),
    ('mm', 'V', 1, 512, 512, 1, 1, 6),
    ('mm', 'V', 1, 512, 512, 2, 0, 4),
    ('e1', 'S', 1, 0, 0),
    ('mm', 'V', 1, 512, 512, 2, 1, 4),
    ('mm', 'V', 1, 512, 512, 3, 0, 5),
    ('W', ('U', 0, 2), 'S', 112, 128),
    ('e1', 'V', 1, 0, 3),
    ('mm', 'V', 1, 512, 512, 3, 1, 5),
    ('e1', 'S', 1, 1, 0),
    ('mm', 'U', 0, 0, 512, 0, 0, 1),
    ('W', ('U', 0, 3), 'V', 0, 48),
    ('mm', 'U', 0, 0, 512, 1, 0, 0),
    ('W', ('U', 0, 3), 'S', 48, 128),
    ('mm', 'U', 0, 0, 512, 2, 0, 2),
    ('Q', ('U', 0, 2), 0, 4),
    ('mm', 'U', 0, 0, 512, 3, 0, 7),
    ('mm', 'U', 0, 0, 512, 0, 1, 1),
    ('e1', 'V', 1, 0, 2),
    ('mm', 'U', 0, 0, 512, 1, 1, 0),
    ('mm', 'U', 0, 0, 512, 2, 1, 2),
    ('e1', 'V', 1, 1, 3),
    ('mm', 'U', 0, 0, 512, 3, 1, 7),
    ('e1', 'S', 1, 1, 1),
    ('mm', 'U', 0, 0, 512, 0, 2, 1),
    ('Q', ('U', 0, 3), 0, 4),
    ('mm', 'U', 0, 0, 512, 1, 2, 0),
    ('e1', 'S', 1, 1, 2),
    ('mm', 'U', 0, 0, 512, 2, 2, 2),
    ('mm', 'U', 0, 0, 512, 3, 2, 7),
    ('W', ('U', 1, 0), 'V', 0, 48),
    ('W', ('U', 1, 0), 'S', 48, 128),
    ('mm', 'U', 0, 0, 512, 0, 3, 1),
    ('mm', 'U', 0, 0, 512, 1, 3, 0),
    ('e2', 0, 0),
    ('mm', 'U', 0, 0, 512, 2, 3, 2),
    ('mm', 'U', 0, 0, 512, 3, 3, 7),
    ('e2', 0, 1),
    ('mm', 'U', 0, 512, 512, 0, 0, 3),
    ('mm', 'U', 0, 512, 512, 0, 1, 3),
    ('e3', 'S', 0, 0),
    ('e2', 0, 3),
    ('mm', 'U', 0, 512, 512, 0, 2, 3),
    ('mm', 'U', 0, 512, 512, 0, 3, 3),
    ('e3', 'S', 0, 1),
    ('e2', 0, 2),
    ('mm', 'U', 0, 512, 512, 1, 0, 5),
    ('mm', 'U', 0, 512, 512, 1, 1, 5),
    ('W', ('U', 1, 1), 'S', 80, 128),
    ('mm', 'U', 0, 512, 512, 1, 2, 5),
    ('e3', 'V', 0, 3),
    ('mm', 'U', 0, 512, 512, 1, 3, 5),
    ('W', ('U', 1, 1), 'V', 0, 80),
    ('mm', 'U', 0, 512, 512, 2, 0, 6),
    ('e3', 'S', 0, 2),
    ('mm', 'U', 0, 512, 512, 2, 1, 6),
    ('W', ('U', 1, 2), 'V', 0, 32),
    ('mm', 'U', 0, 512, 512, 2, 2, 6),
    ('W', ('U', 1, 2), 'S', 32, 128),
    ('mm', 'U', 0, 512, 512, 2, 3, 6),
    ('e2', 1, 1),
    ('T', 0, 0, (0, 1, 2, 3), 4),
    ('e2', 1, 2),
    ('T', 0, 1, (0, 1, 2, 3), 1),
    ('T', 0, 2, (0, 1, 2, 3), 0),
    ('e2', 1, 0),
    ('T', 0, 3, (0, 1, 2, 3), 7),
    ('Q', ('U', 1, 0), 0, 4),
    ('e6', 'S', 0, 0),
    ('mm', 'U', 0, 512, 512, 3, 0, 2),
    ('mm', 'U', 0, 512, 512, 3, 1, 2),
    ('W', ('U', 1, 3), 'V', 0, 48),
    ('W', ('U', 1, 3), 'S', 48, 128),
    ('mm', 'U', 0, 512, 512, 3, 2, 2),
    ('sr', 0, 0),
    ('mm', 'U', 0, 512, 512, 3, 3, 2),
    ('Q', ('U', 1, 1), 0, 4),
    ('mm', 'U', 1, 0, 512, 0, 0, 5),
    ('mm', 'U', 1, 0, 512, 1, 0, 6),
    ('e4', 'V', 0, 1),
    ('mm', 'U', 1, 0, 512, 2, 0, 3),
    ('mm', 'U', 1, 0, 512, 3, 0, 4),
    ('e4', 'S', 0, 0),
    ('Q', ('U', 1, 2), 0, 4),
    ('mm', 'U', 1, 0, 512, 0, 1, 5),
    ('mm', 'U', 1, 0, 512, 1, 1, 6),
    ('Q', ('U', 1, 3), 0, 4),
    ('mm', 'U', 1, 0, 512, 2, 1, 3),
    ('mm', 'U', 1, 0, 512, 3, 1, 4),
    ('e6', 'S', 0, 3),
    ('mm', 'U', 1, 0, 512, 0, 2, 5),
    ('e2', 1, 3),
    ('mm', 'U', 1, 0, 512, 0, 3, 5),
    ('e3', 'S', 1, 0),
    ('e5', 0),
    ('mm', 'U', 1, 0, 512, 1, 2, 6),
    ('sr', 0, 3),
    ('mm', 'U', 1, 0, 512, 1, 3, 6),
    ('e6', 'S', 0, 2),
    ('mm', 'U', 1, 0, 512, 2, 2, 3),
    ('e3', 'V', 1, 2),
    ('sc', 0),
    ('mm', 'U', 1, 0, 512, 2, 3, 3),
    ('e3', 'V', 1, 1),
    ('e3', 'S', 1, 3),
    ('mm', 'U', 1, 0, 512, 3, 2, 4),
    ('e2', 2, 1),
    ('sr', 0, 2),
    ('mm', 'U', 1, 0, 512, 3, 3, 4),
    ('e6', 'S', 0, 1),
    ('mm', 'U', 1, 512, 256, 0, 0, 7),
    ('e2', 2, 2),
    ('mm', 'U', 1, 512, 256, 0, 1, 7),
    ('mm', 'U', 1, 512, 256, 0, 2, 7),
    ('mm', 'U', 1, 512, 256, 0, 3, 7),
    ('e3', 'S', 2, 1),
    ('e2', 2, 3),
    ('T', 1, 0, (0, 1, 2, 3), 2),
    ('sr', 0, 1),
    ('T', 1, 1, (0, 1, 2, 3), 0),
    ('e4', 'S', 1, 1),
    ('e3', 'V', 2, 2),
    ('T', 1, 2, (0, 1, 2, 3), 6),
    ('e2', 2, 0),
    ('T', 1, 3, (0, 1, 2, 3), 1),
    ('e2', 3, 0),
    ('mm', 'U', 1, 512, 256, 1, 0, 3),
    ('mm', 'U', 1, 512, 256, 1, 1, 3),
    ('e3', 'V', 2, 3),
    ('e3', 'S', 2, 0),
    ('mm', 'U', 1, 512, 256, 1, 2, 3),
    ('mm', 'U', 1, 512, 256, 1, 3, 3),
    ('e3', 'V', 3, 0),
    ('mm', 'U', 1, 512, 256, 2, 0, 4),
    ('e6', 'V', 1, 1),
    ('mm', 'U', 1, 512, 256, 2, 1, 4),
    ('e6', 'S', 1, 0),
    ('mm', 'U', 1, 512, 256, 2, 2, 4),
    ('mm', 'U', 1, 512, 256, 2, 3, 4),
    ('e2', 3, 1),
    ('T', 2, 0, (0, 1, 2, 3), 5),
    ('e6', 'S', 1, 3),
    ('sr', 1, 1),
    ('e4', 'V', 2, 1),
    ('sr', 1, 0),
    ('T', 2, 1, (0, 1, 2, 3), 7),
    ('e3', 'S', 3, 1),
    ('T', 2, 2, (0, 1, 2, 3), 0),
    ('sr', 1, 3),
    ('e6', 'V', 2, 0),
    ('e6', 'S', 1, 2),
    ('T', 2, 3, (0, 1, 2, 3), 2),
    ('e2', 3, 2),
    ('mm', 'U', 1, 512, 256, 3, 0, 3),
    ('e6', 'S', 2, 2),
    ('mm', 'U', 1, 512, 256, 3, 1, 3),
    ('sr', 2, 0),
    ('e4', 'V', 1, 0),
    ('mm', 'U', 1, 512, 256, 3, 2, 3),
    ('sr', 1, 2),
    ('mm', 'U', 1, 512, 256, 3, 3, 3),
    ('mm', 'U', 1, 768, 256, 0, 0, 1),
    ('e3', 'S', 3, 2),
    ('mm', 'U', 1, 768, 256, 0, 1, 1),
    ('sr', 2, 2),
    ('mm', 'U', 1, 768, 256, 0, 2, 1),
    ('e6', 'S', 2, 1),
    ('e2', 3, 3),
    ('mm', 'U', 1, 768, 256, 0, 3, 1),
    ('mm', 'U', 1, 768, 256, 1, 0, 5),
    ('e5', 1),
    ('mm', 'U', 1, 768, 256, 1, 1, 5),
    ('mm', 'U', 1, 768, 256, 1, 2, 5),
    ('e3', 'S', 3, 3),
    ('mm', 'U', 1, 768, 256, 1, 3, 5),
    ('mm', 'U', 1, 768, 256, 2, 0, 6),
    ('sr', 2, 1),
    ('e2', 4, 0),
    ('e6', 'S', 2, 3),
    ('mm', 'U', 1, 768, 256, 2, 1, 6),
    ('mm', 'U', 1, 768, 256, 2, 2, 6),
    ('sc', 1),
    ('sp', 0),
    ('e2', 4, 1),
    ('mm', 'U', 1, 768, 256, 2, 3, 6),
    ('mm', 'U', 1, 768, 256, 3, 0, 4),
    ('e4', 'S', 3, 1),
    ('e3', 'V', 4, 0),
    ('mm', 'U', 1, 768, 256, 3, 1, 4),
    ('mm', 'U', 1, 768, 256, 3, 2, 4),
    ('e2', 4, 2),
    ('sr', 2, 3),
    ('mm', 'U', 1, 768, 256, 3, 3, 4),
    ('e4', 'V', 3, 0),
    ('T', 3, 0, (0, 1, 2, 3), 0),
    ('e3', 'S', 4, 1),
    ('e3', 'V', 4, 2),
    ('T', 3, 1, (0, 1, 2, 3), 3),
    ('e2', 4, 3),
    ('e6', 'S', 3, 0),
    ('e5', 3),
    ('T', 4, 0, (0,), 7),
    ('T', 4, 1, (0,), 1),
    ('T', 4, 0, (1,), 7),
    ('T', 4, 1, (1,), 1),
    ('T', 4, 0, (2,), 7),
    ('T', 4, 1, (2,), 1),
    ('e4', 'V', 2, 0),
    ('e6', 'S', 3, 1),
    ('sc', 3),
    ('sr', 3, 0),
    ('e3', 'S', 4, 3),
    ('e5', 2),
    ('sr', 3, 1),
    ('T', 4, 0, (3,), 0),
    ('T', 4, 1, (3,), 0),
    ('e4', 'V', 4, 1),
    ('e6', 'S', 4, 0),
    ('sc', 2),
    ('e4', 'V', 4, 0),
    ('e6', 'S', 4, 1),
    ('e5', 4),
    ('sr', 4, 0),
    ('sc', 4),
    ('sp', 1),
    ('sr', 4, 1),
]


def tile_low_rank_bilinear_fusion_g6_kernel(
    tc, a_words, a_scales, b_words, b_scales, U, V, bias_u, bias_v, bias_f, out_0, out_1, out_2
):
    nc = tc.nc
    with ExitStack() as ctx:
        keep = ctx.enter_context(tc.tile_pool(name="keep", bufs=1))
        stage = ctx.enter_context(tc.tile_pool(name="stage", bufs=3))
        psum = ctx.enter_context(tc.psum_pool(name="psum", bufs=1))
        ctx.enter_context(tc.manual_schedule())

        def bank(i):
            return psum.tile([P, W], F32, name="bank%d" % (i % BANKS))

        bias_rows = keep.tile([P, W], BF16, name="bias_rows", align_bytes=64)
        b_plane = keep.tile([P, S], U8, name="b_plane", align_bytes=64)
        a_plane = keep.tile([P, S], U8, name="a_plane", align_bytes=64)
        ident = keep.tile([P, P], F32, name="ident", align_bytes=64)
        bias = keep.tile([P, 2, 12], F32, name="bias", align_bytes=64)
        nc.vector.memset(b_plane[:].bitcast(I32), 0)
        nc.vector.memset(bias_rows[:].bitcast(I32), 0)
        nc.vector.memset(a_plane[:].bitcast(I32), 0)

        raw, grouped, codes, planes = {}, {}, {}, {}
        act_words = {}

        def load_weight(key):
            name, g, c = key
            src = U if name == "U" else V
            raw[key] = keep.tile([P, PACK, W], BF16, name="raw_%s%d%d" % key, align_bytes=64)
            rows = src[W * c : W * (c + 1), W * g : W * (g + 1)]
            nc.sync.dma_start(out=raw[key][:], in_=rows.rearrange("(p j) r -> p j r", j=PACK))

        def load_words(name, c, h0, h1):
            src = a_words if name == "A" else b_words
            t = keep.tile([P, W * (h1 - h0)], U32, name="words_%s%d%d" % (name, c, h0), align_bytes=64)
            rows = src[c].rearrange("p n t -> p (n t)")[:, PACK * W * h0 : PACK * W * h1]
            nc.sync.dma_start(out=t[:].bitcast(I32), in_=rows.bitcast(I32))
            for h in range(h0, h1):
                act_words[name, c, h] = t[:, W * (h - h0) : W * (h - h0 + 1)]

        def load_plane(eng, plane, src, q):
            n = src.shape[0]
            eng.dma_start(
                out=plane[32 * q : 32 * q + 4 * n, :].bitcast(I32),
                in_=src[:, 4 * q : 4 * q + 4, :].bitcast(I32),
            )

        make_identity(nc, ident[:])
        for i, vec in enumerate((bias_v, bias_u, bias_f)):
            nc.gpsimd.dma_start(out=bias_rows[2 * i : 2 * i + 2, :], in_=vec.rearrange("(g r) -> g r", g=2))
        for q in range(4):
            load_plane(nc.gpsimd, a_plane, a_scales, q)
        for i, key in enumerate(LOADS):
            if key[0] in "UV":
                load_weight(key)
            else:
                load_words(key[0], key[1], key[2], key[2] + 1)
            if i == 1:
                for q in range(4):
                    load_plane(nc.scalar, b_plane, b_scales, q)
        warm = keep.tile([P, 1], F32, name="warm")
        nc.scalar.activation(out=warm[:], in_=ident[:, 0:1], func=IDENTITY)

        held = {}

        def bias_turn(b):
            held["bias"] = bank(b)
            bias_words = bias_rows[:].bitcast(F32)
            for u in range(2):
                nc.tensor.transpose(held["bias"][:, P * u : P * (u + 1)], bias_words[:, u : 2 * P : 2], ident[:])

        def bias_out():
            nc.scalar.activation(
                out=bias[:],
                in_=held["bias"][:, 0 : 2 * P].bitcast(BF16).rearrange("p (u x) -> p u x", u=2)[:, :, 0:12],
                func=IDENTITY,
            )

        def bias_col(i, g, t):
            col = 2 * (2 * i + g) + t % 2
            return bias[:, t // 2, col : col + 1]

        def interleave(key, eng, m0, m1):
            if key not in grouped:
                grouped[key] = stage.tile([P, PACK, P, PACK], BF16, name="grouped", bufs=4, align_bytes=64)
            src = raw[key][:].rearrange("p j (m t) -> p m j t", t=PACK)[:, m0:m1]
            dst = grouped[key][:].rearrange("p t m j -> p m j t")[:, m0:m1]
            if eng == "V":
                nc.vector.tensor_copy(out=dst, in_=src)
            else:
                nc.scalar.copy(out=dst, in_=src)

        def split(key, m):
            if m > 0:
                interleave(key, "V", 0, m)
            if m < P:
                interleave(key, "S", m, P)

        def quantize(key, t0, t1):
            if key not in codes:
                codes[key] = keep.tile([P, W], U32, name="codes_%s%d%d" % key, align_bytes=64)
                planes[key] = keep.tile([P, W], U8, name="plane_%s%d%d" % key, align_bytes=64)
            nc.vector.quantize_mx(
                out=codes[key][:, P * t0 : P * t1].bitcast(FP8X4),
                scales=planes[key][:, P * t0 : P * t1],
                in_=grouped[key][:, t0:t1].rearrange("p t m j -> p (t m j)"),
            )

        acc = {}

        def mm(name, g, s0, n, t, c, b):
            last = 3 if name == "U" else 1
            if c == 0:
                acc[name, g, s0, t] = bank(b)
            act, plane = ("A", a_plane) if name == "U" else ("B", b_plane)
            cols = slice(P * t, P * (t + 1))
            nc.tensor.matmul_mx(
                out=acc[name, g, s0, t][:, 0:n],
                lhsT=codes[name, g, c][:, cols].bitcast(FP8X4),
                lhsT_scale=planes[name, g, c][:, cols],
                rhs=act_words[act, c, s0 // W][:, s0 % W : s0 % W + n].bitcast(FP8X4),
                rhs_scale=plane[4 * c : P, s0 : s0 + n],
                start=(c == 0),
                stop=(c == last),
            )

        right, y, y_bf, turned = {}, {}, {}, {}

        def add_bias(eng, out, in_, col):
            if eng == "S":
                nc.scalar.activation(out=out, in_=in_, func=IDENTITY, bias=col)
            else:
                nc.vector.tensor_scalar(out=out, in0=in_, scalar1=col, scalar2=None, op0=ADD)

        def copy(eng, out, in_):
            if eng == "S":
                nc.scalar.copy(out=out, in_=in_)
            else:
                nc.vector.tensor_copy(out=out, in_=in_)

        def e1(eng, g, h, t):
            right[g, h, t] = keep.tile([P, W], F32, name="right%d%d%d" % (g, h, t), align_bytes=64)
            add_bias(eng, right[g, h, t][:], acc["V", g, W * h, t][:], bias_col(0, g, t))

        def e2(u, t):
            g, s0, n = UNITS[u]
            z = right[g, s0 // W, t][:, s0 % W : s0 % W + n]
            nc.vector.scalar_tensor_tensor(out=z, in0=acc["U", g, s0, t][:, 0:n], scalar=bias_col(1, g, t), in1=z, op0=ADD, op1=MULT)

        def e3(eng, u, t):
            g, s0, n = UNITS[u]
            if u not in y:
                y[u] = keep.tile([P, PACK, n], F32, name="y%d" % u, align_bytes=64)
            add_bias(eng, y[u][:, t, :], right[g, s0 // W, t][:, s0 % W : s0 % W + n], bias_col(2, g, t))

        def turn(u, sb, ts, b):
            if (u, sb) not in turned:
                turned[u, sb] = bank(b)
            for t in ts:
                nc.tensor.transpose(turned[u, sb][:, P * t : P * (t + 1)], y[u][:, t, P * sb : P * (sb + 1)], ident[:])

        y_rows, y_codes, y_plane = {}, {}, {}

        def e6(eng, u, sb):
            y_rows[u, sb] = stage.tile([P, W], F32, name="y_rows", bufs=8, align_bytes=64)
            copy(eng, y_rows[u, sb][:].rearrange("q (m t) -> q m t", t=PACK), turned[u, sb][:].rearrange("q (t m) -> q m t", t=PACK))

        def store_rows(u, sb):
            g, s0, n = UNITS[u]
            nc.sync.dma_start(out=out_0[s0 + P * sb : s0 + P * (sb + 1), W * g : W * (g + 1)], in_=y_rows[u, sb][:])

        def e4(eng, u, half):
            n = UNITS[u][2]
            if u not in y_bf:
                y_bf[u] = keep.tile([P, n, PACK], BF16, name="y_bf%d" % u, align_bytes=64)
            cols = slice(half * n // 2, (half + 1) * n // 2)
            copy(eng, y_bf[u][:, cols, :].rearrange("p (c i) t -> p c t i", i=4), y[u][:, :, cols].rearrange("p t (c i) -> p c t i", i=4))

        def e5(u):
            g, s0, n = UNITS[u]
            y_codes[u] = keep.tile([P, n], U32, name="y_codes%d" % u, align_bytes=64)
            if g not in y_plane:
                y_plane[g] = keep.tile([P, S], U8, name="y_plane%d" % g, align_bytes=64)
            nc.vector.quantize_mx(
                out=y_codes[u][:].bitcast(FP8X4),
                scales=y_plane[g][:, s0 : s0 + n],
                in_=y_bf[u][:].rearrange("p s t -> p (s t)"),
            )

        def store_codes(u):
            g, s0, n = UNITS[u]
            dst = out_1[g].rearrange("p s t -> p (s t)")[:, PACK * s0 : PACK * (s0 + n)]
            nc.sync.dma_start(out=dst.bitcast(I32), in_=y_codes[u][:].bitcast(I32))

        def store_plane(g):
            for q in range(4):
                eng = nc.scalar if g == 1 and q >= 2 else nc.sync
                eng.dma_start(
                        out=out_2[g, 4 * q : 4 * q + 4, :].bitcast(I32), in_=y_plane[g][32 * q : 32 * q + 4, :].bitcast(I32)
                )

        steps = {"W": interleave, "Q": quantize, "mm": mm, "bt": bias_turn, "bo": bias_out, "e1": e1, "e2": e2, "e3": e3,
                 "T": turn, "e6": e6, "sr": store_rows, "e4": e4, "e5": e5, "sc": store_codes, "sp": store_plane}
        for step in PLAN:
            steps[step[0]](*step[1:])
